import numpy as np
import ml_dtypes


def mxq(x, axis, fmt="e4m3"):
    dtype, down = {"e4m3": (ml_dtypes.float8_e4m3fn, 7), "e5m2": (ml_dtypes.float8_e5m2, 14)}[fmt]
    v = np.moveaxis(np.asarray(x, np.float32).astype(ml_dtypes.bfloat16).astype(np.float64), axis, -1)
    blocks = v.reshape(v.shape[:-1] + (-1, 32))
    amax = np.abs(blocks).max(-1, keepdims=True)
    byte = np.maximum(np.where(amax > 0, np.frexp(amax)[1] - 1 + 127, 0) - down, 1)
    scale = np.exp2(byte - 127.0)
    codes = (blocks / scale).astype(np.float32).astype(dtype).astype(np.float64)
    return np.moveaxis((codes * scale).reshape(v.shape), -1, axis)


WIDE = False


def mx_kscale(k):
    if not WIDE:
        return np.ones(k)
    levels = np.array([30, -30])
    if k % 512:
        return np.exp2(np.random.permutation(np.resize(levels, k // 32))).repeat(32)
    a = np.empty((k // 512, 16))
    for p in range(k // 512):
        a[p, :8] = np.random.permutation(np.resize(levels, 8))
        for g in range(8):
            far = levels[np.abs(levels - a[p, g]) >= 10]
            a[p, g + 8] = far[np.random.randint(len(far))]
    return np.exp2(a.ravel()).repeat(32)


def f64(x):
    return np.asarray(x).astype(np.float64)


def striped(idx):
    return np.tile(np.asarray(idx).reshape(-1, 16).T, (8, 1)).astype(np.uint16)


def unstriped(offs):
    return offs[:16].T.reshape(-1).astype(np.int64)


E2M1 = np.array([0.0, 0.5, 1.0, 1.5, 2.0, 3.0, 4.0, 6.0, -0.0, -0.5, -1.0, -1.5, -2.0, -3.0, -4.0, -6.0])


def pack_weight(w, fmt):
    k, n = w.shape
    w = f64(np.asarray(w, np.float32).astype(ml_dtypes.bfloat16)).reshape(k // 32, 32, n)
    amax = np.abs(w).max(1)
    if fmt in ("e4m3", "e5m2"):
        byte = np.frexp(amax)[1] - 1 + 127 - (7 if fmt == "e4m3" else 14)
    else:
        mant, ex = np.frexp(amax / 6.0)
        byte = np.where(mant > 0.5, ex, ex - 1) + 127
    byte = np.clip(np.where(amax > 0, byte, 1), 1, 254)
    scaled = (w * np.exp2(127.0 - byte)[:, None, :]).reshape(k, n).astype(np.float32)
    by_word = np.ascontiguousarray(scaled.reshape(k // 512, 128, 4, n).transpose(0, 1, 3, 2))
    if fmt in ("e4m3", "e5m2"):
        words = by_word.astype(ml_dtypes.float8_e4m3fn if fmt == "e4m3" else ml_dtypes.float8_e5m2).view(np.uint8)
    else:
        c = by_word.astype(ml_dtypes.float4_e2m1fn).view(np.uint8) & 0xF
        words = (c[..., 0::2] | (c[..., 1::2] << 4)).reshape(k // 512, 128, 2 * n)
    return np.ascontiguousarray(words), np.ascontiguousarray(byte.astype(np.uint8).reshape(k // 512, 16, n))


def unpack_weight(words, scales, fmt):
    g, _, n = scales.shape
    words = np.ascontiguousarray(words).reshape(g, 128, n, -1)
    if fmt in ("e4m3", "e5m2"):
        vals = words.view(ml_dtypes.float8_e4m3fn if fmt == "e4m3" else ml_dtypes.float8_e5m2).astype(np.float64)
    else:
        nib = np.empty((g, 128, n, 4), np.uint8)
        nib[..., 0::2] = words & 0xF
        nib[..., 1::2] = words >> 4
        vals = E2M1[nib]
    vals = vals * np.repeat(np.exp2(scales.astype(np.float64) - 127.0), 8, axis=1)[..., None]
    return vals.transpose(0, 1, 3, 2).reshape(g * 512, n)


K, J, N, R, T, V, Q = 512, 512, 256, 256, 1024, 1024, 64


def setup_inputs():
    n = np.random.standard_normal
    idx = np.random.permutation(T)[:J]
    idx2 = np.random.permutation(V)[:J]
    fj = mx_kscale(J)
    fk = mx_kscale(K)
    drp = pack_weight(n((K, R)) * 1 / np.sqrt(K) / fk[:, None], "e5m2")
    return {
        "xf": (n((K, T))).astype(np.float32),
        "ra": (np.random.uniform(0.5, 1.5, (1, J)) * fj).astype(np.float32),
        "lo": (np.random.uniform(-0.3, 0.5, (K, 1))).astype(np.float32),
        "gt": (n((N, V)) * np.exp(0.5 * n((1, V)))).astype(np.float32),
        "rb": (np.random.uniform(0.5, 1.5, (1, J)) / fj).astype(np.float32),
        "cp": (np.random.uniform(0.4, 1.2, (N, 1))).astype(np.float32),
        "fkr": (np.random.uniform(0.5, 1.5, (1, K)) * fk).astype(np.float32),
        "dr_words": drp[0],
        "dr_scales": drp[1],
        "gr1c": (np.random.uniform(0.5, 2.0, (R, 1))).astype(np.float32),
        "offs": striped(idx),
        "offs2": striped(idx2),
    }


def reference(xf, ra, lo, gt, rb, cp, fkr, dr_words, dr_scales, gr1c, offs, offs2):
    idx = unstriped(offs)
    idx2 = unstriped(offs2)
    dru = unpack_weight(dr_words, dr_scales, "e5m2")
    us = np.maximum(f64(xf)[:, idx] - f64(lo), 0.0) * f64(ra)
    ut = us.T
    uj = ut * f64(fkr)
    gs = np.minimum(f64(gt)[:, idx2], f64(cp)) * f64(rb)
    gj = gs.T
    ujq = mxq(uj, 0, "e4m3")
    gjq = mxq(gj, 0, "e5m2")
    w = ujq.T @ gjq
    wq = mxq(w, 0, "e5m2")
    v2 = dru.T @ wq
    wq = v2.reshape(R, Q, N // Q).sum(axis=2)
    y = 0.02 * wq * f64(gr1c)
    return y

@@ -1,0 +1,282 @@
+from contextlib import ExitStack
+
+import concourse.mybir as mybir
+from concourse.masks import make_identity
+
+K, J, N, R, T, V, Q = 512, 512, 256, 256, 1024, 1024, 64
+FLOPS = 2 * J * K * N + 2 * K * R * N
+
+F32 = mybir.dt.float32
+BF16 = mybir.dt.bfloat16
+I32 = mybir.dt.int32
+U32 = mybir.dt.uint32
+U16 = mybir.dt.uint16
+U8 = mybir.dt.uint8
+E4M3 = mybir.dt.float8_e4m3fn_x4
+E5M2 = mybir.dt.float8_e5m2_x4
+ALU = mybir.AluOpType
+COPY = mybir.ActivationFunctionType.Copy
+AX = mybir.AxisListType
+
+P = 128
+PACK = 4
+BANK = 512
+
+
+def tile_list_directions_over_bounded_sums_kernel(
+    tc, xf, ra, lo, gt, rb, cp, fkr, dr_words, dr_scales, gr1c, offs, offs2, out
+):
+    nc = tc.nc
+    with ExitStack() as ctx:
+        sb = ctx.enter_context(tc.tile_pool(name="sb", bufs=1))
+        ps = ctx.enter_context(tc.psum_pool(name="ps", bufs=1))
+
+        def bank(tag, name):
+            return ps.tile([P, BANK], F32, tag=tag, name=name)
+
+        x_list = sb.tile([P, J // 16], U16, name="x_list")
+        g_list = sb.tile([P, J // 16], U16, name="g_list")
+        x_rows = [sb.tile([P, T], F32, name="x_rows%d" % i) for i in range(4)]
+        g_rows = [sb.tile([P, V], F32, name="g_rows%d" % h) for h in range(2)]
+        fk_col = sb.tile([P, PACK], F32, name="fk_col")
+        ra_col = sb.tile([P, PACK], F32, name="ra_col")
+        rb_col = sb.tile([P, PACK], F32, name="rb_col")
+        lo_col = sb.tile([P, PACK], F32, name="lo_col")
+        cp_col = sb.tile([P, 2], F32, name="cp_col")
+        gr_col = sb.tile([P, 2], F32, name="gr_col")
+        dr_codes = sb.tile([P, R], U32, name="dr_codes", align_bytes=64)
+        dr_plane = sb.tile([P, R], U8, name="dr_plane", align_bytes=64)
+        ident = sb.tile([P, P], F32, name="ident")
+
+        xf_by_i = xf.rearrange("(p i) c -> i p c", i=PACK)
+        gt_by_h = gt.rearrange("(p h) c -> h p c", h=2)
+
+        nc.sync.dma_start(g_list[:], offs2)
+        nc.scalar.dma_start(fk_col[:], fkr.rearrange("o (p i) -> p (o i)", i=PACK))
+        nc.sync.dma_start(g_rows[0][:], gt_by_h[0])
+        nc.scalar.dma_start(ra_col[:], ra.rearrange("o (p t) -> p (o t)", t=PACK))
+        nc.sync.dma_start(x_list[:], offs)
+        nc.scalar.dma_start(lo_col[:], lo.rearrange("(p i) o -> p (i o)", i=PACK))
+        nc.sync.dma_start(x_rows[0][:], xf_by_i[0])
+        nc.scalar.dma_start(rb_col[:], rb.rearrange("o (p t) -> p (o t)", t=PACK))
+        nc.sync.dma_start(x_rows[1][:], xf_by_i[1])
+        nc.scalar.dma_start(cp_col[:], cp.rearrange("(p h) o -> p (h o)", h=2))
+        make_identity(nc, ident[:])
+        nc.sync.dma_start(x_rows[2][:], xf_by_i[2])
+        nc.sync.dma_start(x_rows[3][:], xf_by_i[3])
+        nc.sync.dma_start(g_rows[1][:], gt_by_h[1])
+        nc.gpsimd.memset(dr_plane[:].bitcast(I32), 0)
+        nc.sync.dma_start(dr_codes[:].bitcast(I32), dr_words[0].rearrange("p n t -> p (n t)").bitcast(I32))
+        with nc.allow_non_contiguous_dma(reason="one factor a partition"):
+            nc.sync.dma_start(gr_col[:], gr1c.rearrange("(a p) o -> p (a o)", p=P))
+        for quad in range(4):
+            nc.sync.dma_start(dr_plane[32 * quad : 32 * quad + 4, :].bitcast(I32), dr_scales[0, 4 * quad : 4 * quad + 4, :].bitcast(I32))
+
+        rb_bank = bank("b_r", "rb_bank")
+
+        def spread(dst, col):
+            for i in range(PACK):
+                nc.tensor.transpose(dst[:, i * P : (i + 1) * P], col[:, i : i + 1].to_broadcast([P, P]), ident[:])
+
+        neg_lo = sb.tile([P, PACK], F32, name="neg_lo")
+
+        out_scale = sb.tile([P, 2], F32, name="out_scale")
+
+        x_banks = [bank("b_x%d" % i, "x_bank%d" % i) for i in range(PACK)]
+
+        def spread_fk(i):
+            nc.tensor.transpose(x_banks[i][:, :P], fk_col[:, i : i + 1].to_broadcast([P, P]), ident[:])
+
+        factor = [sb.tile([P, P, PACK], F32, name="factor%d" % i) for i in range(PACK)]
+
+        def make_factor(i):
+            nc.vector.tensor_tensor(
+                factor[i][:],
+                x_banks[i][:, :P].unsqueeze(2).to_broadcast([P, P, PACK]),
+                ra_col[:].unsqueeze(1).to_broadcast([P, P, PACK]),
+                ALU.mult,
+            )
+
+        def lay_thresholds(i):
+            for t in range(PACK):
+                nc.tensor.matmul(
+                    x_banks[i][:, t * P : (t + 1) * P],
+                    neg_lo[:, i : i + 1].to_broadcast([P, P]),
+                    ident[:],
+                    start=(t == 0),
+                    stop=False,
+                    is_transpose=True,
+                )
+
+        x_picked = [sb.tile([P, J], F32, name="x_picked%d" % i) for i in range(PACK)]
+        g_picked = [x_picked[1][:], factor[1][:].rearrange("p m t -> p (m t)")]
+        u_bf = [sb.tile([P, J], BF16, name="u_bf%d" % i, align_bytes=64) for i in range(PACK)]
+        u_codes = [sb.tile([P, P], U32, name="u_codes%d" % i, align_bytes=64) for i in range(PACK)]
+        u_plane = [sb.tile([P, P], U8, name="u_plane%d" % i, align_bytes=64) for i in range(PACK)]
+        gs_last = sb.tile([P, J], BF16, name="gs_last")
+        gs_bf = [x_picked[2][:, : J // 2].bitcast(BF16), gs_last[:]]
+        g_bf = [sb.tile([P, J], BF16, name="g_bf%d" % h, align_bytes=64) for h in range(2)]
+        g_codes = [sb.tile([P, P], U32, name="g_codes%d" % h, align_bytes=64) for h in range(2)]
+        g_plane = [sb.tile([P, P], U8, name="g_plane%d" % h, align_bytes=64) for h in range(2)]
+        w_bf = [sb.tile([P, J], BF16, name="w_bf%d" % h, align_bytes=64) for h in range(2)]
+        w_codes = [sb.tile([P, P], U32, name="w_codes%d" % h, align_bytes=64) for h in range(2)]
+        w_plane = [sb.tile([P, P], U8, name="w_plane%d" % h, align_bytes=64) for h in range(2)]
+        g_banks = [bank("b_g%d" % h, "g_bank%d" % h) for h in range(2)]
+
+        def pick_x_scalar(i):
+            nc.scalar.activation(x_picked[i][:], x_rows[i][:].indirect(x_list[:]), COPY)
+
+        def pick_x_vector(i):
+            nc.vector.tensor_copy(
+                x_picked[i][:].rearrange("k (t p) -> k p t", t=PACK), x_rows[i][:].indirect(x_list[:])
+            )
+
+        def turn_x(i, dealt):
+            for t in range(PACK):
+                src = x_picked[i][:, t * P : (t + 1) * P] if dealt else x_picked[i][:, t::PACK]
+                nc.tensor.matmul(
+                    x_banks[i][:, t * P : (t + 1) * P], src, ident[:], start=False, stop=(t == PACK - 1), is_transpose=True
+                )
+
+        def finish_u(i):
+            nc.vector.scalar_tensor_tensor(
+                u_bf[i][:].rearrange("p (m t) -> p m t", t=PACK),
+                x_banks[i][:].rearrange("p (t m) -> p m t", t=PACK),
+                0.0,
+                factor[i][:],
+                ALU.max,
+                ALU.mult,
+            )
+
+        def quant_u(i):
+            nc.vector.quantize_mx(u_codes[i][:].bitcast(E4M3), u_plane[i][:], u_bf[i][:])
+
+        def pick_g_scalar(h):
+            nc.scalar.activation(g_picked[h][:], g_rows[h][:].indirect(g_list[:]), COPY)
+
+        def pick_g_split(h):
+            nc.scalar.activation(g_picked[h][:, : J // 2], g_rows[h][:].indirect(g_list[:, : J // 32]), COPY)
+            nc.vector.tensor_copy(g_picked[h][:, J // 2 :], g_rows[h][:].indirect(g_list[:, J // 32 :]))
+
+        def bound_g(h):
+            nc.vector.scalar_tensor_tensor(
+                gs_bf[h][:].rearrange("n (m t) -> n m t", t=PACK),
+                g_picked[h][:].rearrange("n (m t) -> n m t", t=PACK),
+                cp_col[:, h : h + 1],
+                rb_bank[:].rearrange("n (t m) -> n m t", t=PACK),
+                ALU.min,
+                ALU.mult,
+            )
+
+        def turn_g(h):
+            words = gs_bf[h][:].bitcast(F32)
+            for u in range(2):
+                nc.tensor.transpose(g_banks[h][:, u * P : (u + 1) * P], words[:, u::2], ident[:])
+
+        def weave_g(h):
+            nc.scalar.copy(
+                g_bf[h][:].bitcast(F32).rearrange("p (n u) -> p n u", u=2),
+                g_banks[h][:, : 2 * P].rearrange("p (u n) -> p n u", u=2),
+            )
+
+        def quant_g(h):
+            nc.vector.quantize_mx(g_codes[h][:].bitcast(E5M2), g_plane[h][:], g_bf[h][:])
+
+        w_banks = {}
+
+        def moment(h, i):
+            if h not in w_banks:
+                w_banks[h] = bank(("b_w", "b_x0")[h], "w_bank%d" % h)
+            nc.tensor.matmul_mx(
+                w_banks[h][:, i * P : (i + 1) * P],
+                lhsT=u_codes[i][:].bitcast(E4M3),
+                lhsT_scale=u_plane[i][:],
+                rhs=g_codes[h][:].bitcast(E5M2),
+                rhs_scale=g_plane[h][:],
+                start=True,
+                stop=True,
+            )
+
+        def weave_w(h, on_scalar):
+            dst = w_bf[h][:].rearrange("p (n i) -> p n i", i=PACK)
+            src = w_banks[h][:].rearrange("p (i n) -> p n i", i=PACK)
+            if on_scalar:
+                nc.scalar.copy(dst, src)
+            else:
+                nc.vector.tensor_copy(dst, src)
+
+        def quant_w(h):
+            nc.vector.quantize_mx(w_codes[h][:].bitcast(E5M2), w_plane[h][:], w_bf[h][:])
+
+        v_bank = []
+
+        def directions(h):
+            if not v_bank:
+                v_bank.append(bank("b_x1", "v_bank"))
+            for a in range(2):
+                nc.tensor.matmul_mx(
+                    v_bank[0][:, a * P : (a + 1) * P],
+                    lhsT=dr_codes[:, a * P : (a + 1) * P].bitcast(E5M2),
+                    lhsT_scale=dr_plane[:, a * P : (a + 1) * P],
+                    rhs=w_codes[h][:].bitcast(E5M2),
+                    rhs_scale=w_plane[h][:],
+                    start=(h == 0 and a == 0),
+                    stop=(h == 1 and a == 1),
+                )
+
+        for i in range(PACK):
+            spread_fk(i)
+        nc.gpsimd.tensor_scalar(neg_lo[:], lo_col[:], -1.0, 0.0, ALU.mult, ALU.add)
+        spread(rb_bank, rb_col)
+        pick_g_scalar(0)
+        for i in range(PACK):
+            make_factor(i)
+            lay_thresholds(i)
+        bound_g(0)
+        pick_x_scalar(0)
+        turn_g(0)
+        turn_x(0, False)
+        weave_g(0)
+        pick_x_vector(1)
+        turn_x(1, True)
+        pick_x_scalar(2)
+        finish_u(0)
+        finish_u(1)
+        turn_x(2, False)
+        quant_g(0)
+        quant_u(0)
+        quant_u(1)
+        pick_x_scalar(3)
+        turn_x(3, False)
+        pick_g_split(1)
+        moment(0, 0)
+        moment(0, 1)
+        bound_g(1)
+        turn_g(1)
+        finish_u(2)
+        weave_g(1)
+        finish_u(3)
+        quant_u(2)
+        quant_g(1)
+        quant_u(3)
+        moment(0, 2)
+        moment(1, 0)
+        moment(1, 1)
+        moment(1, 2)
+        moment(0, 3)
+        moment(1, 3)
+        nc.gpsimd.tensor_scalar(out_scale[:], gr_col[:], 0.02, 0.0, ALU.mult, ALU.add)
+        weave_w(0, True)
+        weave_w(1, False)
+        quant_w(0)
+        directions(0)
+        quant_w(1)
+        directions(1)
+
+        sums = sb.tile([P, 2, Q], F32, name="sums")
+        nc.vector.tensor_reduce(
+            sums[:].rearrange("p a q -> p (a q)"), v_bank[0][:, : 2 * P].rearrange("p (c e) -> p c e", e=2), AX.X, ALU.add
+        )
+        result = sb.tile([P, 2, Q], F32, name="result")
+        nc.vector.tensor_tensor(result[:], sums[:], out_scale[:].unsqueeze(2).to_broadcast([P, 2, Q]), ALU.mult)
+        nc.sync.dma_start(out.rearrange("(a p) q -> p a q", p=P), result[:])

@@ -21,6 +21,7 @@ AX = mybir.AxisListType
 P = 128
 PACK = 4
 BANK = 512
+SPLIT = 192
 
 
 def tile_list_directions_over_bounded_sums_kernel(
@@ -38,8 +39,11 @@ def tile_list_directions_over_bounded_sums_kernel(
         g_list = sb.tile([P, J // 16], U16, name="g_list")
         x_rows = [sb.tile([P, T], F32, name="x_rows%d" % i) for i in range(4)]
         g_rows = [sb.tile([P, V], F32, name="g_rows%d" % h) for h in range(2)]
-        fk_col = sb.tile([P, PACK], F32, name="fk_col")
+        x_picked = [sb.tile([P, J], F32, name="x_picked%d" % i) for i in range(PACK)]
+        g_first = sb.tile([P, J], F32, name="g_first")
+        ring = sb.tile([P, J + J // 2], F32, name="ring", align_bytes=64)
         ra_col = sb.tile([P, PACK], F32, name="ra_col")
+        fk_col = g_first[:, :PACK]
         rb_col = sb.tile([P, PACK], F32, name="rb_col")
         lo_col = sb.tile([P, PACK], F32, name="lo_col")
         cp_col = sb.tile([P, 2], F32, name="cp_col")
@@ -51,21 +55,24 @@ def tile_list_directions_over_bounded_sums_kernel(
         xf_by_i = xf.rearrange("(p i) c -> i p c", i=PACK)
         gt_by_h = gt.rearrange("(p h) c -> h p c", h=2)
 
-        nc.sync.dma_start(g_list[:], offs2)
-        nc.scalar.dma_start(fk_col[:], fkr.rearrange("o (p i) -> p (o i)", i=PACK))
-        nc.sync.dma_start(g_rows[0][:], gt_by_h[0])
-        nc.scalar.dma_start(ra_col[:], ra.rearrange("o (p t) -> p (o t)", t=PACK))
         nc.sync.dma_start(x_list[:], offs)
-        nc.scalar.dma_start(lo_col[:], lo.rearrange("(p i) o -> p (i o)", i=PACK))
+        nc.scalar.dma_start(fk_col[:], fkr.rearrange("o (p i) -> p (o i)", i=PACK))
         nc.sync.dma_start(x_rows[0][:], xf_by_i[0])
-        nc.scalar.dma_start(rb_col[:], rb.rearrange("o (p t) -> p (o t)", t=PACK))
+        nc.scalar.dma_start(ra_col[:], ra.rearrange("o (p t) -> p (o t)", t=PACK))
         nc.sync.dma_start(x_rows[1][:], xf_by_i[1])
-        nc.scalar.dma_start(cp_col[:], cp.rearrange("(p h) o -> p (h o)", h=2))
+        nc.scalar.dma_start(lo_col[:], lo.rearrange("(p i) o -> p (i o)", i=PACK))
+        nc.sync.dma_start(g_list[:], offs2)
+        nc.sync.dma_start(rb_col[:], rb.rearrange("o (p t) -> p (o t)", t=PACK))
+        warm = sb.tile([P, 2], F32, name="warm")
+        nc.vector.memset(warm[:, 0:1], 0.0)
+        nc.scalar.activation(warm[:, 1:2], warm[:, 0:1], COPY)
+        nc.sync.dma_start(g_rows[0][:], gt_by_h[0])
+        nc.sync.dma_start(cp_col[:], cp.rearrange("(p h) o -> p (h o)", h=2))
         make_identity(nc, ident[:])
+        nc.gpsimd.memset(dr_plane[:].bitcast(I32), 0)
         nc.sync.dma_start(x_rows[2][:], xf_by_i[2])
         nc.sync.dma_start(x_rows[3][:], xf_by_i[3])
         nc.sync.dma_start(g_rows[1][:], gt_by_h[1])
-        nc.gpsimd.memset(dr_plane[:].bitcast(I32), 0)
         nc.sync.dma_start(dr_codes[:].bitcast(I32), dr_words[0].rearrange("p n t -> p (n t)").bitcast(I32))
         with nc.allow_non_contiguous_dma(reason="one factor a partition"):
             nc.sync.dma_start(gr_col[:], gr1c.rearrange("(a p) o -> p (a o)", p=P))
@@ -80,24 +87,28 @@ def tile_list_directions_over_bounded_sums_kernel(
 
         neg_lo = sb.tile([P, PACK], F32, name="neg_lo")
 
-        out_scale = sb.tile([P, 2], F32, name="out_scale")
 
-        x_banks = [bank("b_x%d" % i, "x_bank%d" % i) for i in range(PACK)]
+        x_banks = {}
+
+        fk_banks = [bank(tag, "fk_" + tag) for tag in ("b_g0", "b_g1", "b_e")]
+        fk_rows = [fk_banks[0][:, :P], fk_banks[1][:, :P], fk_banks[2][:, :P], fk_banks[2][:, P : 2 * P]]
 
         def spread_fk(i):
-            nc.tensor.transpose(x_banks[i][:, :P], fk_col[:, i : i + 1].to_broadcast([P, P]), ident[:])
+            nc.tensor.transpose(fk_rows[i], fk_col[:, i : i + 1].to_broadcast([P, P]), ident[:])
 
-        factor = [sb.tile([P, P, PACK], F32, name="factor%d" % i) for i in range(PACK)]
+        factor = [ring[:, J // 2 :].rearrange("p (m t) -> p m t", t=PACK)]
+        factor.extend([sb.tile([P, P, PACK], F32, name="factor%d" % i)[:] for i in range(1, PACK)])
 
         def make_factor(i):
             nc.vector.tensor_tensor(
                 factor[i][:],
-                x_banks[i][:, :P].unsqueeze(2).to_broadcast([P, P, PACK]),
+                fk_rows[i].unsqueeze(2).to_broadcast([P, P, PACK]),
                 ra_col[:].unsqueeze(1).to_broadcast([P, P, PACK]),
                 ALU.mult,
             )
 
         def lay_thresholds(i):
+            x_banks[i] = bank("b_x%d" % i, "x_bank%d" % i)
             for t in range(PACK):
                 nc.tensor.matmul(
                     x_banks[i][:, t * P : (t + 1) * P],
@@ -108,20 +119,22 @@ def tile_list_directions_over_bounded_sums_kernel(
                     is_transpose=True,
                 )
 
-        x_picked = [sb.tile([P, J], F32, name="x_picked%d" % i) for i in range(PACK)]
-        g_picked = [x_picked[1][:], factor[1][:].rearrange("p m t -> p (m t)")]
-        u_bf = [sb.tile([P, J], BF16, name="u_bf%d" % i, align_bytes=64) for i in range(PACK)]
-        u_codes = [sb.tile([P, P], U32, name="u_codes%d" % i, align_bytes=64) for i in range(PACK)]
-        u_plane = [sb.tile([P, P], U8, name="u_plane%d" % i, align_bytes=64) for i in range(PACK)]
-        gs_last = sb.tile([P, J], BF16, name="gs_last")
-        gs_bf = [x_picked[2][:, : J // 2].bitcast(BF16), gs_last[:]]
+        u_first = sb.tile([P, 2 * J], BF16, name="u_first", align_bytes=64)
+        u_pairs = [u_first[:], ring[:, :J].bitcast(BF16)]
+        u_bf = [u_pairs[i // 2][:, (i % 2) * J : (i % 2 + 1) * J] for i in range(PACK)]
+        g_picked = [g_first[:], ring[:, :J]]
+        u_codes2 = [sb.tile([P, 2 * P], U32, name="u_codes%d" % b, align_bytes=64) for b in range(2)]
+        u_plane2 = [sb.tile([P, 2 * P], U8, name="u_plane%d" % b, align_bytes=64) for b in range(2)]
+        u_codes = [u_codes2[i // 2][:, (i % 2) * P : (i % 2 + 1) * P] for i in range(PACK)]
+        u_plane = [u_plane2[i // 2][:, (i % 2) * P : (i % 2 + 1) * P] for i in range(PACK)]
+        gs_bf = [sb.tile([P, J], BF16, name="gs_bf%d" % h) for h in range(2)]
         g_bf = [sb.tile([P, J], BF16, name="g_bf%d" % h, align_bytes=64) for h in range(2)]
         g_codes = [sb.tile([P, P], U32, name="g_codes%d" % h, align_bytes=64) for h in range(2)]
         g_plane = [sb.tile([P, P], U8, name="g_plane%d" % h, align_bytes=64) for h in range(2)]
         w_bf = [sb.tile([P, J], BF16, name="w_bf%d" % h, align_bytes=64) for h in range(2)]
         w_codes = [sb.tile([P, P], U32, name="w_codes%d" % h, align_bytes=64) for h in range(2)]
         w_plane = [sb.tile([P, P], U8, name="w_plane%d" % h, align_bytes=64) for h in range(2)]
-        g_banks = [bank("b_g%d" % h, "g_bank%d" % h) for h in range(2)]
+        g_banks = {}
 
         def pick_x_scalar(i):
             nc.scalar.activation(x_picked[i][:], x_rows[i][:].indirect(x_list[:]), COPY)
@@ -149,14 +162,20 @@ def tile_list_directions_over_bounded_sums_kernel(
             )
 
         def quant_u(i):
-            nc.vector.quantize_mx(u_codes[i][:].bitcast(E4M3), u_plane[i][:], u_bf[i][:])
+            nc.vector.quantize_mx(u_codes2[i][:].bitcast(E4M3), u_plane2[i][:], u_pairs[i])
+
+        def quant_u_one(i):
+            nc.vector.quantize_mx(u_codes[i].bitcast(E4M3), u_plane[i], u_bf[i])
+
+        def pick_g_vector(h):
+            nc.vector.tensor_copy(g_picked[h][:], g_rows[h][:].indirect(g_list[:]))
 
         def pick_g_scalar(h):
             nc.scalar.activation(g_picked[h][:], g_rows[h][:].indirect(g_list[:]), COPY)
 
         def pick_g_split(h):
-            nc.scalar.activation(g_picked[h][:, : J // 2], g_rows[h][:].indirect(g_list[:, : J // 32]), COPY)
-            nc.vector.tensor_copy(g_picked[h][:, J // 2 :], g_rows[h][:].indirect(g_list[:, J // 32 :]))
+            nc.scalar.activation(g_picked[h][:, :SPLIT], g_rows[h][:].indirect(g_list[:, : SPLIT // 16]), COPY)
+            nc.vector.tensor_copy(g_picked[h][:, SPLIT:], g_rows[h][:].indirect(g_list[:, SPLIT // 16 :]))
 
         def bound_g(h):
             nc.vector.scalar_tensor_tensor(
@@ -169,6 +188,7 @@ def tile_list_directions_over_bounded_sums_kernel(
             )
 
         def turn_g(h):
+            g_banks[h] = bank("b_g%d" % h, "g_bank%d" % h)
             words = gs_bf[h][:].bitcast(F32)
             for u in range(2):
                 nc.tensor.transpose(g_banks[h][:, u * P : (u + 1) * P], words[:, u::2], ident[:])
@@ -186,7 +206,7 @@ def tile_list_directions_over_bounded_sums_kernel(
 
         def moment(h, i):
             if h not in w_banks:
-                w_banks[h] = bank(("b_w", "b_x0")[h], "w_bank%d" % h)
+                w_banks[h] = bank(("b_x2", "b_r")[h], "w_bank%d" % h)
             nc.tensor.matmul_mx(
                 w_banks[h][:, i * P : (i + 1) * P],
                 lhsT=u_codes[i][:].bitcast(E4M3),
@@ -212,60 +232,57 @@ def tile_list_directions_over_bounded_sums_kernel(
 
         def directions(h):
             if not v_bank:
-                v_bank.append(bank("b_x1", "v_bank"))
+                v_bank.extend([bank("b_x0", "v_bank0"), bank("b_x1", "v_bank1")])
             for a in range(2):
                 nc.tensor.matmul_mx(
-                    v_bank[0][:, a * P : (a + 1) * P],
+                    v_bank[a][:, :P],
                     lhsT=dr_codes[:, a * P : (a + 1) * P].bitcast(E5M2),
                     lhsT_scale=dr_plane[:, a * P : (a + 1) * P],
                     rhs=w_codes[h][:].bitcast(E5M2),
                     rhs_scale=w_plane[h][:],
-                    start=(h == 0 and a == 0),
-                    stop=(h == 1 and a == 1),
+                    start=(h == 0),
+                    stop=(h == 1),
                 )
 
         for i in range(PACK):
             spread_fk(i)
         nc.gpsimd.tensor_scalar(neg_lo[:], lo_col[:], -1.0, 0.0, ALU.mult, ALU.add)
+        for i in range(PACK):
+            lay_thresholds(i)
         spread(rb_bank, rb_col)
-        pick_g_scalar(0)
         for i in range(PACK):
             make_factor(i)
-            lay_thresholds(i)
-        bound_g(0)
-        pick_x_scalar(0)
-        turn_g(0)
+        for i in range(PACK):
+            pick_x_scalar(i)
+        pick_g_vector(0)
         turn_x(0, False)
-        weave_g(0)
-        pick_x_vector(1)
-        turn_x(1, True)
-        pick_x_scalar(2)
+        turn_x(1, False)
         finish_u(0)
+        bound_g(0)
         finish_u(1)
+        turn_g(0)
         turn_x(2, False)
-        quant_g(0)
-        quant_u(0)
-        quant_u(1)
-        pick_x_scalar(3)
         turn_x(3, False)
         pick_g_split(1)
-        moment(0, 0)
-        moment(0, 1)
+        weave_g(0)
+        quant_u(0)
         bound_g(1)
         turn_g(1)
+        quant_g(0)
         finish_u(2)
         weave_g(1)
         finish_u(3)
-        quant_u(2)
+        quant_u_one(2)
         quant_g(1)
-        quant_u(3)
+        quant_u_one(3)
+        moment(0, 0)
+        moment(0, 1)
         moment(0, 2)
         moment(1, 0)
         moment(1, 1)
         moment(1, 2)
         moment(0, 3)
         moment(1, 3)
-        nc.gpsimd.tensor_scalar(out_scale[:], gr_col[:], 0.02, 0.0, ALU.mult, ALU.add)
         weave_w(0, True)
         weave_w(1, False)
         quant_w(0)
@@ -274,9 +291,9 @@ def tile_list_directions_over_bounded_sums_kernel(
         directions(1)
 
         sums = sb.tile([P, 2, Q], F32, name="sums")
-        nc.vector.tensor_reduce(
-            sums[:].rearrange("p a q -> p (a q)"), v_bank[0][:, : 2 * P].rearrange("p (c e) -> p c e", e=2), AX.X, ALU.add
-        )
         result = sb.tile([P, 2, Q], F32, name="result")
-        nc.vector.tensor_tensor(result[:], sums[:], out_scale[:].unsqueeze(2).to_broadcast([P, 2, Q]), ALU.mult)
+        for a in range(2):
+            nc.vector.tensor_reduce(sums[:, a, :], v_bank[a][:, :P].rearrange("p (c e) -> p c e", e=2), AX.X, ALU.add)
+        for a in range(2):
+            nc.vector.tensor_scalar(result[:, a, :], sums[:, a, :], gr_col[:, a : a + 1], 0.02, ALU.mult, ALU.mult)
         nc.sync.dma_start(out.rearrange("(a p) q -> p a q", p=P), result[:])

from contextlib import ExitStack

import concourse.mybir as mybir
from concourse.masks import make_identity

K, J, N, R, T, V, Q = 512, 512, 256, 256, 1024, 1024, 64
FLOPS = 2 * J * K * N + 2 * K * R * N

F32 = mybir.dt.float32
BF16 = mybir.dt.bfloat16
I32 = mybir.dt.int32
U32 = mybir.dt.uint32
U16 = mybir.dt.uint16
U8 = mybir.dt.uint8
E4M3 = mybir.dt.float8_e4m3fn_x4
E5M2 = mybir.dt.float8_e5m2_x4
ALU = mybir.AluOpType
COPY = mybir.ActivationFunctionType.Copy
AX = mybir.AxisListType

P = 128
PACK = 4
BANK = 512
SPLIT = 192


def tile_list_directions_over_bounded_sums_kernel(
    tc, xf, ra, lo, gt, rb, cp, fkr, dr_words, dr_scales, gr1c, offs, offs2, out
):
    nc = tc.nc
    with ExitStack() as ctx:
        sb = ctx.enter_context(tc.tile_pool(name="sb", bufs=1))
        ps = ctx.enter_context(tc.psum_pool(name="ps", bufs=1))

        def bank(tag, name):
            return ps.tile([P, BANK], F32, tag=tag, name=name)

        x_list = sb.tile([P, J // 16], U16, name="x_list")
        g_list = sb.tile([P, J // 16], U16, name="g_list")
        x_rows = [sb.tile([P, T], F32, name="x_rows%d" % i) for i in range(4)]
        g_rows = [sb.tile([P, V], F32, name="g_rows%d" % h) for h in range(2)]
        x_picked = [sb.tile([P, J], F32, name="x_picked%d" % i) for i in range(PACK)]
        g_first = sb.tile([P, J], F32, name="g_first")
        ring = sb.tile([P, J + J // 2], F32, name="ring", align_bytes=64)
        ra_col = sb.tile([P, PACK], F32, name="ra_col")
        fk_col = g_first[:, :PACK]
        rb_col = sb.tile([P, PACK], F32, name="rb_col")
        lo_col = sb.tile([P, PACK], F32, name="lo_col")
        cp_col = sb.tile([P, 2], F32, name="cp_col")
        gr_col = sb.tile([P, 2], F32, name="gr_col")
        dr_codes = sb.tile([P, R], U32, name="dr_codes", align_bytes=64)
        dr_plane = sb.tile([P, R], U8, name="dr_plane", align_bytes=64)
        ident = sb.tile([P, P], F32, name="ident")

        xf_by_i = xf.rearrange("(p i) c -> i p c", i=PACK)
        gt_by_h = gt.rearrange("(p h) c -> h p c", h=2)

        nc.sync.dma_start(x_list[:], offs)
        nc.scalar.dma_start(fk_col[:], fkr.rearrange("o (p i) -> p (o i)", i=PACK))
        nc.sync.dma_start(x_rows[0][:], xf_by_i[0])
        nc.scalar.dma_start(ra_col[:], ra.rearrange("o (p t) -> p (o t)", t=PACK))
        nc.sync.dma_start(x_rows[1][:], xf_by_i[1])
        nc.scalar.dma_start(lo_col[:], lo.rearrange("(p i) o -> p (i o)", i=PACK))
        nc.sync.dma_start(g_list[:], offs2)
        nc.sync.dma_start(rb_col[:], rb.rearrange("o (p t) -> p (o t)", t=PACK))
        warm = sb.tile([P, 2], F32, name="warm")
        nc.vector.memset(warm[:, 0:1], 0.0)
        nc.scalar.activation(warm[:, 1:2], warm[:, 0:1], COPY)
        nc.sync.dma_start(g_rows[0][:], gt_by_h[0])
        nc.sync.dma_start(cp_col[:], cp.rearrange("(p h) o -> p (h o)", h=2))
        make_identity(nc, ident[:])
        nc.gpsimd.memset(dr_plane[:].bitcast(I32), 0)
        nc.sync.dma_start(x_rows[2][:], xf_by_i[2])
        nc.sync.dma_start(x_rows[3][:], xf_by_i[3])
        nc.sync.dma_start(g_rows[1][:], gt_by_h[1])
        nc.sync.dma_start(dr_codes[:].bitcast(I32), dr_words[0].rearrange("p n t -> p (n t)").bitcast(I32))
        with nc.allow_non_contiguous_dma(reason="one factor a partition"):
            nc.sync.dma_start(gr_col[:], gr1c.rearrange("(a p) o -> p (a o)", p=P))
        for quad in range(4):
            nc.sync.dma_start(dr_plane[32 * quad : 32 * quad + 4, :].bitcast(I32), dr_scales[0, 4 * quad : 4 * quad + 4, :].bitcast(I32))

        rb_bank = bank("b_r", "rb_bank")

        def spread(dst, col):
            for i in range(PACK):
                nc.tensor.transpose(dst[:, i * P : (i + 1) * P], col[:, i : i + 1].to_broadcast([P, P]), ident[:])

        neg_lo = sb.tile([P, PACK], F32, name="neg_lo")


        x_banks = {}

        fk_banks = [bank(tag, "fk_" + tag) for tag in ("b_g0", "b_g1", "b_e")]
        fk_rows = [fk_banks[0][:, :P], fk_banks[1][:, :P], fk_banks[2][:, :P], fk_banks[2][:, P : 2 * P]]

        def spread_fk(i):
            nc.tensor.transpose(fk_rows[i], fk_col[:, i : i + 1].to_broadcast([P, P]), ident[:])

        factor = [ring[:, J // 2 :].rearrange("p (m t) -> p m t", t=PACK)]
        factor.extend([sb.tile([P, P, PACK], F32, name="factor%d" % i)[:] for i in range(1, PACK)])

        def make_factor(i):
            nc.vector.tensor_tensor(
                factor[i][:],
                fk_rows[i].unsqueeze(2).to_broadcast([P, P, PACK]),
                ra_col[:].unsqueeze(1).to_broadcast([P, P, PACK]),
                ALU.mult,
            )

        def lay_thresholds(i):
            x_banks[i] = bank("b_x%d" % i, "x_bank%d" % i)
            for t in range(PACK):
                nc.tensor.matmul(
                    x_banks[i][:, t * P : (t + 1) * P],
                    neg_lo[:, i : i + 1].to_broadcast([P, P]),
                    ident[:],
                    start=(t == 0),
                    stop=False,
                    is_transpose=True,
                )

        u_first = sb.tile([P, 2 * J], BF16, name="u_first", align_bytes=64)
        u_pairs = [u_first[:], ring[:, :J].bitcast(BF16)]
        u_bf = [u_pairs[i // 2][:, (i % 2) * J : (i % 2 + 1) * J] for i in range(PACK)]
        g_picked = [g_first[:], ring[:, :J]]
        u_codes2 = [sb.tile([P, 2 * P], U32, name="u_codes%d" % b, align_bytes=64) for b in range(2)]
        u_plane2 = [sb.tile([P, 2 * P], U8, name="u_plane%d" % b, align_bytes=64) for b in range(2)]
        u_codes = [u_codes2[i // 2][:, (i % 2) * P : (i % 2 + 1) * P] for i in range(PACK)]
        u_plane = [u_plane2[i // 2][:, (i % 2) * P : (i % 2 + 1) * P] for i in range(PACK)]
        gs_bf = [sb.tile([P, J], BF16, name="gs_bf%d" % h) for h in range(2)]
        g_bf = [sb.tile([P, J], BF16, name="g_bf%d" % h, align_bytes=64) for h in range(2)]
        g_codes = [sb.tile([P, P], U32, name="g_codes%d" % h, align_bytes=64) for h in range(2)]
        g_plane = [sb.tile([P, P], U8, name="g_plane%d" % h, align_bytes=64) for h in range(2)]
        w_bf = [sb.tile([P, J], BF16, name="w_bf%d" % h, align_bytes=64) for h in range(2)]
        w_codes = [sb.tile([P, P], U32, name="w_codes%d" % h, align_bytes=64) for h in range(2)]
        w_plane = [sb.tile([P, P], U8, name="w_plane%d" % h, align_bytes=64) for h in range(2)]
        g_banks = {}

        def pick_x_scalar(i):
            nc.scalar.activation(x_picked[i][:], x_rows[i][:].indirect(x_list[:]), COPY)

        def pick_x_vector(i):
            nc.vector.tensor_copy(
                x_picked[i][:].rearrange("k (t p) -> k p t", t=PACK), x_rows[i][:].indirect(x_list[:])
            )

        def turn_x(i, dealt):
            for t in range(PACK):
                src = x_picked[i][:, t * P : (t + 1) * P] if dealt else x_picked[i][:, t::PACK]
                nc.tensor.matmul(
                    x_banks[i][:, t * P : (t + 1) * P], src, ident[:], start=False, stop=(t == PACK - 1), is_transpose=True
                )

        def finish_u(i):
            nc.vector.scalar_tensor_tensor(
                u_bf[i][:].rearrange("p (m t) -> p m t", t=PACK),
                x_banks[i][:].rearrange("p (t m) -> p m t", t=PACK),
                0.0,
                factor[i][:],
                ALU.max,
                ALU.mult,
            )

        def quant_u(i):
            nc.vector.quantize_mx(u_codes2[i][:].bitcast(E4M3), u_plane2[i][:], u_pairs[i])

        def quant_u_one(i):
            nc.vector.quantize_mx(u_codes[i].bitcast(E4M3), u_plane[i], u_bf[i])

        def pick_g_vector(h):
            nc.vector.tensor_copy(g_picked[h][:], g_rows[h][:].indirect(g_list[:]))

        def pick_g_scalar(h):
            nc.scalar.activation(g_picked[h][:], g_rows[h][:].indirect(g_list[:]), COPY)

        def pick_g_split(h):
            nc.scalar.activation(g_picked[h][:, :SPLIT], g_rows[h][:].indirect(g_list[:, : SPLIT // 16]), COPY)
            nc.vector.tensor_copy(g_picked[h][:, SPLIT:], g_rows[h][:].indirect(g_list[:, SPLIT // 16 :]))

        def bound_g(h):
            nc.vector.scalar_tensor_tensor(
                gs_bf[h][:].rearrange("n (m t) -> n m t", t=PACK),
                g_picked[h][:].rearrange("n (m t) -> n m t", t=PACK),
                cp_col[:, h : h + 1],
                rb_bank[:].rearrange("n (t m) -> n m t", t=PACK),
                ALU.min,
                ALU.mult,
            )

        def turn_g(h):
            g_banks[h] = bank("b_g%d" % h, "g_bank%d" % h)
            words = gs_bf[h][:].bitcast(F32)
            for u in range(2):
                nc.tensor.transpose(g_banks[h][:, u * P : (u + 1) * P], words[:, u::2], ident[:])

        def weave_g(h):
            nc.scalar.copy(
                g_bf[h][:].bitcast(F32).rearrange("p (n u) -> p n u", u=2),
                g_banks[h][:, : 2 * P].rearrange("p (u n) -> p n u", u=2),
            )

        def quant_g(h):
            nc.vector.quantize_mx(g_codes[h][:].bitcast(E5M2), g_plane[h][:], g_bf[h][:])

        w_banks = {}

        def moment(h, i):
            if h not in w_banks:
                w_banks[h] = bank(("b_x2", "b_r")[h], "w_bank%d" % h)
            nc.tensor.matmul_mx(
                w_banks[h][:, i * P : (i + 1) * P],
                lhsT=u_codes[i][:].bitcast(E4M3),
                lhsT_scale=u_plane[i][:],
                rhs=g_codes[h][:].bitcast(E5M2),
                rhs_scale=g_plane[h][:],
                start=True,
                stop=True,
            )

        def weave_w(h, on_scalar):
            dst = w_bf[h][:].rearrange("p (n i) -> p n i", i=PACK)
            src = w_banks[h][:].rearrange("p (i n) -> p n i", i=PACK)
            if on_scalar:
                nc.scalar.copy(dst, src)
            else:
                nc.vector.tensor_copy(dst, src)

        def quant_w(h):
            nc.vector.quantize_mx(w_codes[h][:].bitcast(E5M2), w_plane[h][:], w_bf[h][:])

        v_bank = []

        def directions(h):
            if not v_bank:
                v_bank.extend([bank("b_x0", "v_bank0"), bank("b_x1", "v_bank1")])
            for a in range(2):
                nc.tensor.matmul_mx(
                    v_bank[a][:, :P],
                    lhsT=dr_codes[:, a * P : (a + 1) * P].bitcast(E5M2),
                    lhsT_scale=dr_plane[:, a * P : (a + 1) * P],
                    rhs=w_codes[h][:].bitcast(E5M2),
                    rhs_scale=w_plane[h][:],
                    start=(h == 0),
                    stop=(h == 1),
                )

        for i in range(PACK):
            spread_fk(i)
        nc.gpsimd.tensor_scalar(neg_lo[:], lo_col[:], -1.0, 0.0, ALU.mult, ALU.add)
        for i in range(PACK):
            lay_thresholds(i)
        spread(rb_bank, rb_col)
        for i in range(PACK):
            make_factor(i)
        for i in range(PACK):
            pick_x_scalar(i)
        pick_g_vector(0)
        turn_x(0, False)
        turn_x(1, False)
        finish_u(0)
        bound_g(0)
        finish_u(1)
        turn_g(0)
        turn_x(2, False)
        turn_x(3, False)
        pick_g_split(1)
        weave_g(0)
        quant_u(0)
        bound_g(1)
        turn_g(1)
        quant_g(0)
        finish_u(2)
        weave_g(1)
        finish_u(3)
        quant_u_one(2)
        quant_g(1)
        quant_u_one(3)
        moment(0, 0)
        moment(0, 1)
        moment(0, 2)
        moment(1, 0)
        moment(1, 1)
        moment(1, 2)
        moment(0, 3)
        moment(1, 3)
        weave_w(0, True)
        weave_w(1, False)
        quant_w(0)
        directions(0)
        quant_w(1)
        directions(1)

        sums = sb.tile([P, 2, Q], F32, name="sums")
        result = sb.tile([P, 2, Q], F32, name="result")
        for a in range(2):
            nc.vector.tensor_reduce(sums[:, a, :], v_bank[a][:, :P].rearrange("p (c e) -> p c e", e=2), AX.X, ALU.add)
        for a in range(2):
            nc.vector.tensor_scalar(result[:, a, :], sums[:, a, :], gr_col[:, a : a + 1], 0.02, ALU.mult, ALU.mult)
        nc.sync.dma_start(out.rearrange("(a p) q -> p a q", p=P), result[:])
